import numpy as np
import ml_dtypes


def mxq(x, axis, fmt="e4m3"):
    dtype, down = {"e4m3": (ml_dtypes.float8_e4m3fn, 7), "e5m2": (ml_dtypes.float8_e5m2, 14)}[fmt]
    v = np.moveaxis(np.asarray(x, np.float32).astype(ml_dtypes.bfloat16).astype(np.float64), axis, -1)
    blocks = v.reshape(v.shape[:-1] + (-1, 32))
    amax = np.abs(blocks).max(-1, keepdims=True)
    byte = np.maximum(np.where(amax > 0, np.frexp(amax)[1] - 1 + 127, 0) - down, 1)
    scale = np.exp2(byte - 127.0)
    codes = (blocks / scale).astype(np.float32).astype(dtype).astype(np.float64)
    return np.moveaxis((codes * scale).reshape(v.shape), -1, axis)


WIDE = False


def mx_kscale(k):
    if not WIDE:
        return np.ones(k)
    levels = np.array([10, -10, 5, -5, 0])
    if k % 512:
        return np.exp2(np.random.permutation(np.resize(levels, k // 32))).repeat(32)
    a = np.empty((k // 512, 16))
    for p in range(k // 512):
        a[p, :8] = np.random.permutation(np.resize(levels, 8))
        for g in range(8):
            far = levels[np.abs(levels - a[p, g]) >= 10]
            a[p, g + 8] = far[np.random.randint(len(far))]
    return np.exp2(a.ravel()).repeat(32)


BF16 = ml_dtypes.bfloat16


def bf(x):
    return np.asarray(x, np.float32).astype(BF16)


def f64(x):
    return np.asarray(x).astype(np.float64)

E4M3FN = np.array([(-1.0 if i & 128 else 1.0) * ((1.0 + (i & 7) / 8.0) * 2.0 ** (((i >> 3) & 15) - 7) if i & 120 else (i & 7) * 2.0 ** -9) for i in range(256)])


def e4m3fn_bytes(y):
    return np.clip(np.asarray(y, np.float64), -448.0, 448.0).astype(np.float32).astype(ml_dtypes.float8_e4m3fn).view(np.uint8)


def e4m3fn_values(b):
    return E4M3FN[b]

def planes(Y):
    n, m = Y.shape
    b = f64(bf(Y)).reshape(n // 32, 32, m)
    amax = np.abs(b).max(1)
    byte = np.clip(np.where(amax > 0, np.frexp(amax)[1] - 1 + 127 - 7, 1), 1, 254)
    codes = (b * np.exp2(127.0 - byte)[:, None, :]).reshape(n, m).astype(np.float32).astype(ml_dtypes.float8_e4m3fn).view(np.uint8)
    words = codes.reshape(n // 512, 128, 4, m).transpose(0, 1, 3, 2)
    return np.ascontiguousarray(words), np.ascontiguousarray(byte.astype(np.uint8).reshape(n // 512, 16, m))


D, R1, R2, H, O, BK = 1024, 512, 512, 3, 1024, 128
TOP = 448.0

def setup_inputs():
    rn = np.random.randn
    t1, t2 = mx_kscale(R1), mx_kscale(R2)
    W = rn(D, H * O)
    A = 0.5 * rn(D, R1) / np.sqrt(R1) / t1[None, :]
    B = rn(R1 * H, R2) / np.sqrt(R2) / t2[None, :]
    C = rn(R2, O) * t2[:, None]
    W_scale = (np.abs(W).reshape(D // BK, BK, H * O // BK, BK).max(axis=(1, 3)) / TOP).astype(np.float32)
    A_scale = (np.abs(A).max(axis=0, keepdims=True) / TOP).astype(np.float32)
    B_scale = (np.abs(B).max(axis=0, keepdims=True) / TOP).astype(np.float32)
    C_scale = (np.abs(C).max(axis=1, keepdims=True) / TOP).astype(np.float32)
    W_wide = np.repeat(np.repeat(f64(W_scale), BK, axis=0), BK, axis=1)
    return {
        "W_bytes": e4m3fn_bytes(W / W_wide), "W_scale": W_scale,
        "A_bytes": e4m3fn_bytes(A / f64(A_scale)), "A_scale": A_scale,
        "B_bytes": e4m3fn_bytes(B / f64(B_scale)), "B_scale": B_scale,
        "C_bytes": e4m3fn_bytes(C / f64(C_scale)), "C_scale": C_scale,
        "bond_gain": bf((1 + 0.2 * rn(R1, 1)) * t1[:, None]),
        "in_gain": bf(np.exp(0.8 * rn(D, 1))),
        "out_gain": bf(1 + 0.1 * rn(1, H * O)),
    }

def reference(W_bytes, W_scale, A_bytes, A_scale, B_bytes, B_scale, C_bytes, C_scale, bond_gain, in_gain, out_gain):
    W = e4m3fn_values(W_bytes) * np.repeat(np.repeat(f64(W_scale), BK, axis=0), BK, axis=1)
    A = e4m3fn_values(A_bytes) * f64(A_scale)
    B = e4m3fn_values(B_bytes) * f64(B_scale)
    C = e4m3fn_values(C_bytes) * f64(C_scale)
    U = (mxq(B, 1, "e4m3") @ mxq(C, 0, "e4m3")).reshape(R1, H * O)
    V = U * f64(bond_gain)
    P = mxq(A, 1, "e4m3") @ mxq(V, 0, "e4m3")
    y = (W + P) * f64(in_gain) * f64(out_gain)
    Y = y
    words, scales = planes(Y)
    return y, words, scales

@@ -1,0 +1,367 @@
+from contextlib import ExitStack
+
+import concourse.mybir as mybir
+from concourse.masks import make_identity
+
+D_IN, RANK, HEADS, D_OUT, BLOCK = 1024, 512, 3, 1024, 128
+COLS = HEADS * D_OUT
+FLOPS = 2 * (HEADS * RANK) * RANK * D_OUT + 2 * D_IN * RANK * COLS
+
+F32 = mybir.dt.float32
+BF16 = mybir.dt.bfloat16
+U32 = mybir.dt.uint32
+I32 = mybir.dt.int32
+U8 = mybir.dt.uint8
+FP8 = mybir.dt.float8_e4m3fn
+FP8X4 = mybir.dt.float8_e4m3fn_x4
+MULT = mybir.AluOpType.mult
+ADD = mybir.AluOpType.add
+COPY = mybir.ActivationFunctionType.Copy
+
+P = 128
+PACK = 4
+CHUNK = 512
+GROUPS = D_IN // CHUNK
+CHUNKS = COLS // CHUNK
+STEPS = GROUPS * CHUNKS
+WIDE = PACK * CHUNK
+
+
+def tile_tensor_train_weight_merge_b6_kernel(
+    tc, W_bytes, W_scale, A_bytes, A_scale, B_bytes, B_scale, C_bytes, C_scale,
+    bond_gain, in_gain, out_gain, out_0, out_1, out_2,
+):
+    nc = tc.nc
+    with ExitStack() as ctx:
+        keep = ctx.enter_context(tc.tile_pool(name="keep", bufs=1))
+        work = ctx.enter_context(tc.tile_pool(name="work", bufs=3))
+        ypool = ctx.enter_context(tc.tile_pool(name="ypool", bufs=8))
+        psum = ctx.enter_context(tc.psum_pool(name="psum", bufs=7))
+        gain_psum = ctx.enter_context(tc.psum_pool(name="gain_psum", bufs=1))
+        ctx.enter_context(tc.manual_schedule())
+
+        ident = keep.tile([P, P], F32, name="ident")
+        make_identity(nc, ident[:])
+
+        def load(engine, name, shape, dtype, src):
+            dst = keep.tile(shape, dtype, name=name)
+            engine.dma_start(out=dst[:], in_=src)
+            return dst
+
+        def load_c(n):
+            src = C_bytes[:, n * CHUNK:(n + 1) * CHUNK].rearrange("(p t) o -> p t o", t=PACK)
+            return load(nc.sync, "c_raw%d" % n, [P, PACK, CHUNK], U8, src)
+
+        def load_b(h):
+            src = B_bytes.rearrange("(p t h) k -> h p t k", t=PACK, h=HEADS)[h]
+            return load(nc.sync, "b_raw%d" % h, [P, PACK, RANK], U8, src)
+
+        def load_a(g):
+            src = A_bytes[g * CHUNK:(g + 1) * CHUNK, :].rearrange("(p t) k -> p t k", t=PACK)
+            return load(nc.sync, "a_raw%d" % g, [P, PACK, RANK], U8, src)
+
+        def load_w(g, h):
+            src = W_bytes[g * CHUNK:(g + 1) * CHUNK, h * D_OUT:(h + 1) * D_OUT]
+            return load(nc.sync, "w_raw%d_%d" % (g, h), [P, PACK, D_OUT], U8,
+                        src.rearrange("(p t) n -> p t n", t=PACK))
+
+        c_raw, b_raw, a_raw, w_raw = {}, {}, {}, {}
+        c_raw[0] = load_c(0)
+        b_raw[0] = load_b(0)
+        c_sc = load(nc.scalar, "c_sc", [P, PACK], F32, C_scale.rearrange("(p t) o -> p (t o)", t=PACK))
+        b_sc = load(nc.scalar, "b_sc", [P, PACK], F32, B_scale.rearrange("o (p t) -> p (o t)", t=PACK))
+        a_raw[0] = load_a(0)
+        a_sc = load(nc.scalar, "a_sc", [P, PACK], F32, A_scale.rearrange("o (p t) -> p (o t)", t=PACK))
+        bond = load(nc.scalar, "bond", [P, PACK], BF16, bond_gain.rearrange("(p t) o -> p (t o)", t=PACK))
+        a_raw[1] = load_a(1)
+        c_raw[1] = load_c(1)
+        w_sc = load(nc.sync, "w_sc", [P, GROUPS * PACK * (COLS // BLOCK)], F32,
+                    W_scale.rearrange("u v -> (u v)").partition_broadcast(P))
+        row_gain = load(nc.sync, "row_gain", [P, GROUPS, PACK], BF16,
+                        in_gain.rearrange("(g p t) o -> p g (t o)", p=P, t=PACK))
+        w_raw[0, 0] = load_w(0, 0)
+        col_gain_p = load(nc.sync, "col_gain_p", [P, CHUNKS, PACK], BF16,
+                          out_gain.rearrange("o (c p t) -> p (o c) t", p=P, t=PACK))
+        w_raw[1, 0] = load_w(1, 0)
+        b_raw[1] = load_b(1)
+        col_gain = load(nc.sync, "col_gain", [P, COLS], BF16,
+                        out_gain.rearrange("o n -> (o n)").partition_broadcast(P))
+        b_raw[2] = load_b(2)
+        for h in range(1, HEADS):
+            for g in range(GROUPS):
+                w_raw[g, h] = load_w(g, h)
+
+        nblk = COLS // BLOCK
+        w_fac = keep.tile([P, GROUPS, PACK, nblk], F32, name="w_fac")
+        w_sc_v = w_sc[:].rearrange("p (g q v) -> p g q v", g=GROUPS, q=PACK)
+        for q in range(4):
+            rows = slice(32 * q, 32 * q + 32)
+            nc.gpsimd.tensor_tensor(
+                out=w_fac[rows],
+                in0=w_sc_v[rows, :, q:q + 1, :].to_broadcast([32, GROUPS, PACK, nblk]),
+                in1=row_gain[rows].unsqueeze(3).to_broadcast([32, GROUPS, PACK, nblk]),
+                op=MULT,
+            )
+        col_gain_f = keep.tile([P, CHUNKS * PACK], F32, name="col_gain_f")
+        nc.gpsimd.tensor_copy(out=col_gain_f[:], in_=col_gain_p[:].rearrange("p c t -> p (c t)"))
+
+        def new_wide():
+            return work.tile([P, WIDE], BF16, name="wide", align_bytes=64)
+
+        def new_grouped():
+            return work.tile([P, WIDE], BF16, name="grouped", bufs=4, align_bytes=64)
+
+        def new_bank():
+            return psum.tile([P, CHUNK], F32, name="bank")
+
+        def quantize(name, grouped, pool):
+            codes = pool.tile([P, CHUNK], U32, name=name + "_codes", align_bytes=64)
+            scales = pool.tile([P, CHUNK], U8, name=name + "_scales", align_bytes=64)
+            nc.vector.quantize_mx(out=codes[:].bitcast(FP8X4), scales=scales[:], in_=grouped[:])
+            return codes, scales
+
+        def interleave_views(grouped, planes):
+            dst = grouped.rearrange("p (c i t) -> p c t i", i=4, t=PACK)
+            src = planes.rearrange("p t (c i) -> p c t i", i=4)
+            return dst, src
+
+        def widen_rows(raw, first=False):
+            wide = new_wide()
+            src = raw[:].rearrange("p t k -> p (t k)").bitcast(FP8)
+            if first:
+                nc.scalar.activation(out=wide[:], in_=src, func=COPY)
+            else:
+                nc.scalar.copy(out=wide[:], in_=src)
+            return wide
+
+        def turn(wide, half):
+            bank = new_bank()
+            words = wide[:].bitcast(F32)
+            for j in range(2):
+                w0 = 256 * (2 * half + j)
+                for u in range(2):
+                    c0 = 256 * u + P * j
+                    nc.tensor.transpose(bank[:, c0:c0 + P], words[:, w0 + u:w0 + 256:2], ident[:])
+            return bank
+
+        def scale_turned(bank, scale, grouped, half):
+            nc.vector.tensor_tensor(
+                out=grouped[:, 1024 * half:1024 * (half + 1)].rearrange("p (r u e) -> p r u e", u=2, e=2),
+                in0=bank[:].bitcast(BF16).rearrange("p (u r e) -> p r u e", u=2, e=2),
+                in1=scale[:].rearrange("p (u e) -> p u e", e=2).unsqueeze(1).to_broadcast([P, 256, 2, 2]),
+                op=MULT,
+            )
+
+        a_q, b_q, c_q, v_q = {}, {}, {}, {}
+
+        def mx(out, lhs, lcols, rhs, rcols):
+            nc.tensor.matmul_mx(
+                out=out, lhsT=lhs[0][:, lcols].bitcast(FP8X4), lhsT_scale=lhs[1][:, lcols],
+                rhs=rhs[0][:, rcols].bitcast(FP8X4), rhs_scale=rhs[1][:, rcols], start=True, stop=True,
+            )
+
+        def u_matmuls(c, j):
+            bank = new_bank()
+            for t in range(PACK):
+                mx(bank[:, P * t:P * (t + 1)], b_q[c // 2], slice(P * t, P * (t + 1)),
+                   c_q[c % 2], slice(P * j, P * (j + 1)))
+            return bank
+
+        def u_out(bank, grouped, j):
+            nc.vector.tensor_tensor(
+                out=grouped[:, CHUNK * j:CHUNK * (j + 1)].rearrange("p (o t) -> p o t", t=PACK),
+                in0=bank[:].rearrange("p (t o) -> p o t", t=PACK),
+                in1=bond[:].unsqueeze(1).to_broadcast([P, P, PACK]),
+                op=MULT,
+            )
+
+        y, p_bank, gain_bank, y_grouped = {}, {}, {}, {}
+
+        def widen_w(s):
+            c, g = divmod(s, GROUPS)
+            y[s] = ypool.tile([P, PACK, CHUNK], F32, name="y")
+            raw = w_raw[g, c // 2]
+            for t in range(PACK):
+                for v in range(CHUNK // BLOCK):
+                    c0 = (c % 2) * CHUNK + v * BLOCK
+                    blk = c * (CHUNK // BLOCK) + v
+                    nc.scalar.activation(
+                        out=y[s][:, t, v * BLOCK:(v + 1) * BLOCK], in_=raw[:, t, c0:c0 + BLOCK].bitcast(FP8),
+                        func=COPY, scale=w_fac[:, g, t, blk:blk + 1],
+                    )
+
+        def p_matmul(s, t):
+            c, g = divmod(s, GROUPS)
+            p_bank[s, t] = new_bank()
+            mx(p_bank[s, t][:], a_q[g], slice(P * t, P * (t + 1)), v_q[c], slice(0, CHUNK))
+
+        def add_p(s, t):
+            g = s % GROUPS
+            nc.vector.scalar_tensor_tensor(
+                out=y[s][:, t, :], in0=p_bank[s, t][:], scalar=row_gain[:, g, t:t + 1], in1=y[s][:, t, :],
+                op0=MULT, op1=ADD,
+            )
+
+        def spread_gain(c):
+            gain_bank[c] = gain_psum.tile([P, CHUNK], F32, name="gain_bank")
+            for t in range(PACK):
+                col = col_gain_f[:, PACK * c + t:PACK * c + t + 1].to_broadcast([P, P])
+                nc.tensor.transpose(gain_bank[c][:, t:CHUNK:PACK], col, ident[:])
+
+        def gain_gpsimd(s, lo, hi):
+            c = s // GROUPS
+            gain = col_gain[:, c * CHUNK:(c + 1) * CHUNK].unsqueeze(1).to_broadcast([P, hi - lo, CHUNK])
+            nc.gpsimd.tensor_tensor(out=y[s][:, lo:hi, :], in0=y[s][:, lo:hi, :], in1=gain, op=MULT)
+
+        def gain_vector(s, t):
+            nc.vector.tensor_tensor(out=y[s][:, t, :], in0=y[s][:, t, :], in1=gain_bank[s // GROUPS][:], op=MULT)
+
+        def store_y(s):
+            c, g = divmod(s, GROUPS)
+            dst = out_0[g * CHUNK:(g + 1) * CHUNK, c * CHUNK:(c + 1) * CHUNK]
+            nc.sync.dma_start(out=dst.rearrange("(p t) n -> p t n", t=PACK), in_=y[s][:])
+
+        def round_y(s, split=False):
+            y_grouped[s] = work.tile([P, WIDE], BF16, name="y_grouped", align_bytes=64)
+            dst, src = interleave_views(y_grouped[s][:], y[s][:])
+            if split:
+                nc.scalar.copy(out=dst[:, 0:48], in_=src[:, 0:48])
+                nc.vector.tensor_copy(out=dst[:, 48:128], in_=src[:, 48:128])
+            else:
+                nc.scalar.copy(out=dst, in_=src)
+
+        early_cols = COLS - CHUNK
+        y_scales_early = keep.tile([P, GROUPS, early_cols], U8, name="y_scales_early", align_bytes=64)
+        y_scales_last = keep.tile([P, GROUPS, CHUNK], U8, name="y_scales_last", align_bytes=64)
+
+        def quantize_y(s):
+            c, g = divmod(s, GROUPS)
+            codes = work.tile([P, CHUNK], U32, name="y_codes", align_bytes=64)
+            if c < CHUNKS - 1:
+                scales = y_scales_early[:, g, c * CHUNK:(c + 1) * CHUNK]
+            else:
+                scales = y_scales_last[:, g, :]
+            nc.vector.quantize_mx(out=codes[:].bitcast(FP8X4), scales=scales, in_=y_grouped[s][:])
+            dst = out_1[g, :, c * CHUNK:(c + 1) * CHUNK, :].rearrange("p m t -> p (m t)").bitcast(I32)
+            nc.sync.dma_start(out=dst, in_=codes[:].bitcast(I32))
+
+        def store_scales(engine, scales, c0, c1):
+            for q in range(4):
+                dst = out_2[:, 4 * q:4 * q + 4, c0:c1].rearrange("g r n -> r g n").bitcast(I32)
+                engine.dma_start(out=dst, in_=scales[32 * q:32 * q + 4].bitcast(I32))
+
+        wide_b0 = widen_rows(b_raw[0], first=True)
+        planes = new_wide()
+        for t in range(PACK):
+            nc.vector.tensor_scalar(out=planes[:, t * CHUNK:(t + 1) * CHUNK], in0=c_raw[0][:, t, :].bitcast(FP8),
+                                    scalar1=c_sc[:, t:t + 1], scalar2=None, op0=MULT)
+        grouped_c = new_grouped()
+        dst, src = interleave_views(grouped_c[:], planes[:].rearrange("p (t o) -> p t o", t=PACK))
+        nc.vector.tensor_copy(out=dst, in_=src)
+        banks_b = [turn(wide_b0, half) for half in range(2)]
+        wide_a0 = widen_rows(a_raw[0])
+        banks_a = [turn(wide_a0, half) for half in range(2)]
+        wide_a1 = widen_rows(a_raw[1])
+        grouped_b = new_grouped()
+        grouped_a = new_grouped()
+        scale_turned(banks_b[0], b_sc, grouped_b, 0)
+        c_q[0] = quantize("c0", grouped_c, keep)
+        scale_turned(banks_b[1], b_sc, grouped_b, 1)
+        scale_turned(banks_a[0], a_sc, grouped_a, 0)
+        b_q[0] = quantize("b0", grouped_b, keep)
+        banks_u = [u_matmuls(0, j) for j in range(4)]
+        scale_turned(banks_a[1], a_sc, grouped_a, 1)
+        banks_a = [turn(wide_a1, half) for half in range(2)]
+
+        planes = new_wide()
+        for t in range(PACK):
+            nc.scalar.activation(out=planes[:, t * CHUNK:(t + 1) * CHUNK], in_=c_raw[1][:, t, :].bitcast(FP8),
+                                 func=COPY, scale=c_sc[:, t:t + 1])
+        grouped_c = new_grouped()
+        dst, src = interleave_views(grouped_c[:], planes[:].rearrange("p (t o) -> p t o", t=PACK))
+        nc.scalar.copy(out=dst, in_=src)
+        widen_w(0)
+        widen_w(1)
+
+        grouped_v = new_grouped()
+        u_out(banks_u[0], grouped_v, 0)
+        a_q[0] = quantize("a0", grouped_a, keep)
+        for j in range(1, 4):
+            u_out(banks_u[j], grouped_v, j)
+        grouped_a = new_grouped()
+        scale_turned(banks_a[0], a_sc, grouped_a, 0)
+        v_q[0] = quantize("v", grouped_v, work)
+        for t in range(PACK):
+            p_matmul(0, t)
+        spread_gain(0)
+        scale_turned(banks_a[1], a_sc, grouped_a, 1)
+        c_q[1] = quantize("c1", grouped_c, keep)
+        add_p(0, 0)
+        add_p(0, 1)
+
+        u_jobs = {0: [(1, j) for j in range(4)], 2: [(2, j) for j in range(4)]}
+        for c in range(3, CHUNKS):
+            u_jobs[2 * c - 3] = [(c, 0), (c, 1)]
+            u_jobs[2 * c - 2] = [(c, 2), (c, 3)]
+        b_jobs = {1: [(1, 0), (1, 1)], 3: [(2, 0)], 4: [(2, 1)]}
+        wide_b, grouped_bs, grouped_vs = {}, {}, {}
+
+        for s in range(STEPS):
+            last = s == STEPS - 1
+            lo = 0 if s < 9 else (2 if last else 1)
+            if s >= 1:
+                store_y(s - 1)
+            if s >= 2:
+                quantize_y(s - 2)
+            if s == 0:
+                a_q[1] = quantize("a1", grouped_a, keep)
+            if s == 2:
+                b_q[1] = quantize("b1", grouped_bs[1], keep)
+            if s == 5:
+                b_q[2] = quantize("b2", grouped_bs[2], keep)
+            if s % 2 == 1 and (s + 1) // 2 < CHUNKS:
+                v_q[(s + 1) // 2] = quantize("v", grouped_vs[(s + 1) // 2], work)
+            if last:
+                store_scales(nc.sync, y_scales_early, 0, early_cols)
+            if s >= 1:
+                round_y(s - 1)
+            if s == 0:
+                wide_b[1] = widen_rows(b_raw[1])
+            if s + 2 < STEPS:
+                widen_w(s + 2)
+            if s == 0:
+                wide_b[2] = widen_rows(b_raw[2])
+
+            jobs = [("u", c, j) for c, j in u_jobs.get(s, [])] + [("b", h, j) for h, j in b_jobs.get(s, [])]
+            banks = [u_matmuls(c, j) if kind == "u" else turn(wide_b[c], j) for kind, c, j in jobs]
+            add_p(s, 2)
+            gain_gpsimd(s, lo, 3)
+            add_p(s, 3)
+            if not last:
+                p_matmul(s + 1, 0)
+                p_matmul(s + 1, 1)
+            for t in range(lo):
+                gain_vector(s, t)
+            for n, (kind, c, j) in enumerate(jobs):
+                if kind == "u":
+                    if j == 0:
+                        grouped_vs[c] = new_grouped()
+                    u_out(banks[n], grouped_vs[c], j)
+                else:
+                    if j == 0:
+                        grouped_bs[c] = new_grouped()
+                    scale_turned(banks[n], b_sc, grouped_bs[c], j)
+            gain_vector(s, 3)
+            if not last:
+                p_matmul(s + 1, 2)
+                p_matmul(s + 1, 3)
+                if s % 2 == 1:
+                    spread_gain((s + 1) // 2)
+                add_p(s + 1, 0)
+                add_p(s + 1, 1)
+
+        store_y(STEPS - 1)
+        quantize_y(STEPS - 2)
+        round_y(STEPS - 1, split=True)
+        quantize_y(STEPS - 1)
+        store_scales(nc.scalar, y_scales_last, early_cols, COLS)

@@ -25,6 +25,9 @@ GROUPS = D_IN // CHUNK
 CHUNKS = COLS // CHUNK
 STEPS = GROUPS * CHUNKS
 WIDE = PACK * CHUNK
+GATE = 128
+SHARE = {4: 480, 2: 384, 0: 288}
+LAST_SHARE = 128
 
 
 def tile_tensor_train_weight_merge_b6_kernel(
@@ -52,13 +55,13 @@ def tile_tensor_train_weight_merge_b6_kernel(
             src = C_bytes[:, n * CHUNK:(n + 1) * CHUNK].rearrange("(p t) o -> p t o", t=PACK)
             return load(nc.sync, "c_raw%d" % n, [P, PACK, CHUNK], U8, src)
 
-        def load_b(h):
-            src = B_bytes.rearrange("(p t h) k -> h p t k", t=PACK, h=HEADS)[h]
-            return load(nc.sync, "b_raw%d" % h, [P, PACK, RANK], U8, src)
+        def load_b(h, half):
+            src = B_bytes.rearrange("(p t h) k -> h p t k", t=PACK, h=HEADS)[h][:, 2 * half:2 * half + 2, :]
+            return load(nc.sync, "b_raw%d_%d" % (h, half), [P, 2, RANK], U8, src)
 
-        def load_a(g):
+        def load_a(g, half):
             src = A_bytes[g * CHUNK:(g + 1) * CHUNK, :].rearrange("(p t) k -> p t k", t=PACK)
-            return load(nc.sync, "a_raw%d" % g, [P, PACK, RANK], U8, src)
+            return load(nc.sync, "a_raw%d_%d" % (g, half), [P, 2, RANK], U8, src[:, 2 * half:2 * half + 2, :])
 
         def load_w(g, h):
             src = W_bytes[g * CHUNK:(g + 1) * CHUNK, h * D_OUT:(h + 1) * D_OUT]
@@ -66,14 +69,17 @@ def tile_tensor_train_weight_merge_b6_kernel(
                         src.rearrange("(p t) n -> p t n", t=PACK))
 
         c_raw, b_raw, a_raw, w_raw = {}, {}, {}, {}
+        b_raw[0, 0] = load_b(0, 0)
         c_raw[0] = load_c(0)
-        b_raw[0] = load_b(0)
         c_sc = load(nc.scalar, "c_sc", [P, PACK], F32, C_scale.rearrange("(p t) o -> p (t o)", t=PACK))
         b_sc = load(nc.scalar, "b_sc", [P, PACK], F32, B_scale.rearrange("o (p t) -> p (o t)", t=PACK))
-        a_raw[0] = load_a(0)
+        b_raw[0, 1] = load_b(0, 1)
+        a_raw[0, 0] = load_a(0, 0)
+        a_raw[0, 1] = load_a(0, 1)
         a_sc = load(nc.scalar, "a_sc", [P, PACK], F32, A_scale.rearrange("o (p t) -> p (o t)", t=PACK))
         bond = load(nc.scalar, "bond", [P, PACK], BF16, bond_gain.rearrange("(p t) o -> p (t o)", t=PACK))
-        a_raw[1] = load_a(1)
+        a_raw[1, 0] = load_a(1, 0)
+        a_raw[1, 1] = load_a(1, 1)
         c_raw[1] = load_c(1)
         w_sc = load(nc.sync, "w_sc", [P, GROUPS * PACK * (COLS // BLOCK)], F32,
                     W_scale.rearrange("u v -> (u v)").partition_broadcast(P))
@@ -83,10 +89,12 @@ def tile_tensor_train_weight_merge_b6_kernel(
         col_gain_p = load(nc.sync, "col_gain_p", [P, CHUNKS, PACK], BF16,
                           out_gain.rearrange("o (c p t) -> p (o c) t", p=P, t=PACK))
         w_raw[1, 0] = load_w(1, 0)
-        b_raw[1] = load_b(1)
+        b_raw[1, 0] = load_b(1, 0)
+        b_raw[1, 1] = load_b(1, 1)
         col_gain = load(nc.sync, "col_gain", [P, COLS], BF16,
                         out_gain.rearrange("o n -> (o n)").partition_broadcast(P))
-        b_raw[2] = load_b(2)
+        b_raw[2, 0] = load_b(2, 0)
+        b_raw[2, 1] = load_b(2, 1)
         for h in range(1, HEADS):
             for g in range(GROUPS):
                 w_raw[g, h] = load_w(g, h)
@@ -106,7 +114,7 @@ def tile_tensor_train_weight_merge_b6_kernel(
         nc.gpsimd.tensor_copy(out=col_gain_f[:], in_=col_gain_p[:].rearrange("p c t -> p (c t)"))
 
         def new_wide():
-            return work.tile([P, WIDE], BF16, name="wide", align_bytes=64)
+            return work.tile([P, WIDE], BF16, name="wide", bufs=2, align_bytes=64)
 
         def new_grouped():
             return work.tile([P, WIDE], BF16, name="grouped", bufs=4, align_bytes=64)
@@ -126,7 +134,7 @@ def tile_tensor_train_weight_merge_b6_kernel(
             return dst, src
 
         def widen_rows(raw, first=False):
-            wide = new_wide()
+            wide = work.tile([P, WIDE // 2], BF16, name="wide_rows", bufs=6, align_bytes=64)
             src = raw[:].rearrange("p t k -> p (t k)").bitcast(FP8)
             if first:
                 nc.scalar.activation(out=wide[:], in_=src, func=COPY)
@@ -134,14 +142,13 @@ def tile_tensor_train_weight_merge_b6_kernel(
                 nc.scalar.copy(out=wide[:], in_=src)
             return wide
 
-        def turn(wide, half):
+        def turn(wide):
             bank = new_bank()
             words = wide[:].bitcast(F32)
             for j in range(2):
-                w0 = 256 * (2 * half + j)
                 for u in range(2):
                     c0 = 256 * u + P * j
-                    nc.tensor.transpose(bank[:, c0:c0 + P], words[:, w0 + u:w0 + 256:2], ident[:])
+                    nc.tensor.transpose(bank[:, c0:c0 + P], words[:, 256 * j + u:256 * (j + 1):2], ident[:])
             return bank
 
         def scale_turned(bank, scale, grouped, half):
@@ -195,11 +202,11 @@ def tile_tensor_train_weight_merge_b6_kernel(
             p_bank[s, t] = new_bank()
             mx(p_bank[s, t][:], a_q[g], slice(P * t, P * (t + 1)), v_q[c], slice(0, CHUNK))
 
-        def add_p(s, t):
+        def add_p(s, t, c0=0, c1=CHUNK):
             g = s % GROUPS
             nc.vector.scalar_tensor_tensor(
-                out=y[s][:, t, :], in0=p_bank[s, t][:], scalar=row_gain[:, g, t:t + 1], in1=y[s][:, t, :],
-                op0=MULT, op1=ADD,
+                out=y[s][:, t, c0:c1], in0=p_bank[s, t][:, c0:c1], scalar=row_gain[:, g, t:t + 1],
+                in1=y[s][:, t, c0:c1], op0=MULT, op1=ADD,
             )
 
         def spread_gain(c):
@@ -208,27 +215,25 @@ def tile_tensor_train_weight_merge_b6_kernel(
                 col = col_gain_f[:, PACK * c + t:PACK * c + t + 1].to_broadcast([P, P])
                 nc.tensor.transpose(gain_bank[c][:, t:CHUNK:PACK], col, ident[:])
 
-        def gain_gpsimd(s, lo, hi):
+        def gain_gpsimd(s, c0, c1):
             c = s // GROUPS
-            gain = col_gain[:, c * CHUNK:(c + 1) * CHUNK].unsqueeze(1).to_broadcast([P, hi - lo, CHUNK])
-            nc.gpsimd.tensor_tensor(out=y[s][:, lo:hi, :], in0=y[s][:, lo:hi, :], in1=gain, op=MULT)
+            gain = col_gain[:, c * CHUNK + c0:c * CHUNK + c1].unsqueeze(1).to_broadcast([P, PACK, c1 - c0])
+            nc.gpsimd.tensor_tensor(out=y[s][:, :, c0:c1], in0=y[s][:, :, c0:c1], in1=gain, op=MULT)
 
-        def gain_vector(s, t):
-            nc.vector.tensor_tensor(out=y[s][:, t, :], in0=y[s][:, t, :], in1=gain_bank[s // GROUPS][:], op=MULT)
+        def gain_vector(s, c0, c1):
+            gain = gain_bank[s // GROUPS][:, c0:c1].unsqueeze(1).to_broadcast([P, PACK, c1 - c0])
+            nc.vector.tensor_tensor(out=y[s][:, :, c0:c1], in0=y[s][:, :, c0:c1], in1=gain, op=MULT)
 
-        def store_y(s):
+        def store_y(s, c0=0, c1=CHUNK):
             c, g = divmod(s, GROUPS)
-            dst = out_0[g * CHUNK:(g + 1) * CHUNK, c * CHUNK:(c + 1) * CHUNK]
-            nc.sync.dma_start(out=dst.rearrange("(p t) n -> p t n", t=PACK), in_=y[s][:])
+            dst = out_0[g * CHUNK:(g + 1) * CHUNK, c * CHUNK + c0:c * CHUNK + c1]
+            nc.sync.dma_start(out=dst.rearrange("(p t) n -> p t n", t=PACK), in_=y[s][:, :, c0:c1])
 
-        def round_y(s, split=False):
-            y_grouped[s] = work.tile([P, WIDE], BF16, name="y_grouped", align_bytes=64)
+        def round_y(copy, s, c0=0, c1=CHUNK):
+            if s not in y_grouped:
+                y_grouped[s] = work.tile([P, WIDE], BF16, name="y_grouped", align_bytes=64)
             dst, src = interleave_views(y_grouped[s][:], y[s][:])
-            if split:
-                nc.scalar.copy(out=dst[:, 0:48], in_=src[:, 0:48])
-                nc.vector.tensor_copy(out=dst[:, 48:128], in_=src[:, 48:128])
-            else:
-                nc.scalar.copy(out=dst, in_=src)
+            copy(out=dst[:, c0 // 4:c1 // 4], in_=src[:, c0 // 4:c1 // 4])
 
         early_cols = COLS - CHUNK
         y_scales_early = keep.tile([P, GROUPS, early_cols], U8, name="y_scales_early", align_bytes=64)
@@ -250,7 +255,7 @@ def tile_tensor_train_weight_merge_b6_kernel(
                 dst = out_2[:, 4 * q:4 * q + 4, c0:c1].rearrange("g r n -> r g n").bitcast(I32)
                 engine.dma_start(out=dst, in_=scales[32 * q:32 * q + 4].bitcast(I32))
 
-        wide_b0 = widen_rows(b_raw[0], first=True)
+        wide_b0 = [widen_rows(b_raw[0, half], first=(half == 0)) for half in range(2)]
         planes = new_wide()
         for t in range(PACK):
             nc.vector.tensor_scalar(out=planes[:, t * CHUNK:(t + 1) * CHUNK], in0=c_raw[0][:, t, :].bitcast(FP8),
@@ -258,10 +263,10 @@ def tile_tensor_train_weight_merge_b6_kernel(
         grouped_c = new_grouped()
         dst, src = interleave_views(grouped_c[:], planes[:].rearrange("p (t o) -> p t o", t=PACK))
         nc.vector.tensor_copy(out=dst, in_=src)
-        banks_b = [turn(wide_b0, half) for half in range(2)]
-        wide_a0 = widen_rows(a_raw[0])
-        banks_a = [turn(wide_a0, half) for half in range(2)]
-        wide_a1 = widen_rows(a_raw[1])
+        banks_b = [turn(wide_b0[half]) for half in range(2)]
+        wide_a0 = [widen_rows(a_raw[0, half]) for half in range(2)]
+        banks_a = [turn(wide_a0[half]) for half in range(2)]
+        wide_a1 = [widen_rows(a_raw[1, half]) for half in range(2)]
         grouped_b = new_grouped()
         grouped_a = new_grouped()
         scale_turned(banks_b[0], b_sc, grouped_b, 0)
@@ -271,7 +276,7 @@ def tile_tensor_train_weight_merge_b6_kernel(
         b_q[0] = quantize("b0", grouped_b, keep)
         banks_u = [u_matmuls(0, j) for j in range(4)]
         scale_turned(banks_a[1], a_sc, grouped_a, 1)
-        banks_a = [turn(wide_a1, half) for half in range(2)]
+        banks_a = [turn(wide_a1[half]) for half in range(2)]
 
         planes = new_wide()
         for t in range(PACK):
@@ -296,8 +301,9 @@ def tile_tensor_train_weight_merge_b6_kernel(
         spread_gain(0)
         scale_turned(banks_a[1], a_sc, grouped_a, 1)
         c_q[1] = quantize("c1", grouped_c, keep)
-        add_p(0, 0)
-        add_p(0, 1)
+        for t in range(PACK - 1):
+            add_p(0, t)
+        add_p(0, PACK - 1, GATE, CHUNK)
 
         u_jobs = {0: [(1, j) for j in range(4)], 2: [(2, j) for j in range(4)]}
         for c in range(3, CHUNKS):
@@ -308,11 +314,10 @@ def tile_tensor_train_weight_merge_b6_kernel(
 
         for s in range(STEPS):
             last = s == STEPS - 1
-            lo = 0 if s < 9 else (2 if last else 1)
-            if s >= 1:
+            if last:
+                store_y(s - 1, 0, SHARE[0])
+            elif s >= 1:
                 store_y(s - 1)
-            if s >= 2:
-                quantize_y(s - 2)
             if s == 0:
                 a_q[1] = quantize("a1", grouped_a, keep)
             if s == 2:
@@ -321,27 +326,28 @@ def tile_tensor_train_weight_merge_b6_kernel(
                 b_q[2] = quantize("b2", grouped_bs[2], keep)
             if s % 2 == 1 and (s + 1) // 2 < CHUNKS:
                 v_q[(s + 1) // 2] = quantize("v", grouped_vs[(s + 1) // 2], work)
+            if s >= 2:
+                quantize_y(s - 2)
             if last:
                 store_scales(nc.sync, y_scales_early, 0, early_cols)
             if s >= 1:
-                round_y(s - 1)
+                round_y(nc.scalar.copy, s - 1)
             if s == 0:
-                wide_b[1] = widen_rows(b_raw[1])
+                wide_b[1] = [widen_rows(b_raw[1, half]) for half in range(2)]
             if s + 2 < STEPS:
                 widen_w(s + 2)
             if s == 0:
-                wide_b[2] = widen_rows(b_raw[2])
+                wide_b[2] = [widen_rows(b_raw[2, half]) for half in range(2)]
 
             jobs = [("u", c, j) for c, j in u_jobs.get(s, [])] + [("b", h, j) for h, j in b_jobs.get(s, [])]
-            banks = [u_matmuls(c, j) if kind == "u" else turn(wide_b[c], j) for kind, c, j in jobs]
-            add_p(s, 2)
-            gain_gpsimd(s, lo, 3)
-            add_p(s, 3)
+            weight = sum(1 if kind == "u" else 2 for kind, c, j in jobs)
+            share = LAST_SHARE if last else SHARE[weight]
+            banks = [u_matmuls(c, j) if kind == "u" else turn(wide_b[c][j]) for kind, c, j in jobs]
+            add_p(s, PACK - 1, 0, GATE)
+            gain_gpsimd(s, 0, share)
             if not last:
-                p_matmul(s + 1, 0)
-                p_matmul(s + 1, 1)
-            for t in range(lo):
-                gain_vector(s, t)
+                for t in range(PACK - 1):
+                    p_matmul(s + 1, t)
             for n, (kind, c, j) in enumerate(jobs):
                 if kind == "u":
                     if j == 0:
@@ -351,17 +357,25 @@ def tile_tensor_train_weight_merge_b6_kernel(
                     if j == 0:
                         grouped_bs[c] = new_grouped()
                     scale_turned(banks[n], b_sc, grouped_bs[c], j)
-            gain_vector(s, 3)
-            if not last:
-                p_matmul(s + 1, 2)
-                p_matmul(s + 1, 3)
+            if last:
+                gain_vector(s, 256, CHUNK)
+                store_y(s, 256, CHUNK)
+                gain_vector(s, share, 256)
+            else:
+                gain_vector(s, share, CHUNK)
+                if s == STEPS - 2:
+                    store_y(s, share, CHUNK)
+                p_matmul(s + 1, PACK - 1)
                 if s % 2 == 1:
                     spread_gain((s + 1) // 2)
-                add_p(s + 1, 0)
-                add_p(s + 1, 1)
+                for t in range(PACK - 1):
+                    add_p(s + 1, t)
+                add_p(s + 1, PACK - 1, GATE, CHUNK)
 
-        store_y(STEPS - 1)
+        store_y(STEPS - 1, 0, 256)
+        round_y(nc.scalar.copy, STEPS - 1, 384, 512)
+        round_y(nc.vector.tensor_copy, STEPS - 1, 128, 384)
+        round_y(nc.vector.tensor_copy, STEPS - 1, 0, 128)
         quantize_y(STEPS - 2)
-        round_y(STEPS - 1, split=True)
         quantize_y(STEPS - 1)
         store_scales(nc.scalar, y_scales_last, early_cols, COLS)

@@ -69,8 +69,8 @@ def tile_tensor_train_weight_merge_b6_kernel(
                         src.rearrange("(p t) n -> p t n", t=PACK))
 
         c_raw, b_raw, a_raw, w_raw = {}, {}, {}, {}
-        b_raw[0, 0] = load_b(0, 0)
         c_raw[0] = load_c(0)
+        b_raw[0, 0] = load_b(0, 0)
         c_sc = load(nc.scalar, "c_sc", [P, PACK], F32, C_scale.rearrange("(p t) o -> p (t o)", t=PACK))
         b_sc = load(nc.scalar, "b_sc", [P, PACK], F32, B_scale.rearrange("o (p t) -> p (o t)", t=PACK))
         b_raw[0, 1] = load_b(0, 1)
@@ -235,19 +235,21 @@ def tile_tensor_train_weight_merge_b6_kernel(
             dst, src = interleave_views(y_grouped[s][:], y[s][:])
             copy(out=dst[:, c0 // 4:c1 // 4], in_=src[:, c0 // 4:c1 // 4])
 
-        early_cols = COLS - CHUNK
+        early_cols = COLS - 2 * CHUNK
         y_scales_early = keep.tile([P, GROUPS, early_cols], U8, name="y_scales_early", align_bytes=64)
-        y_scales_last = keep.tile([P, GROUPS, CHUNK], U8, name="y_scales_last", align_bytes=64)
+        y_scales_last = keep.tile([P, GROUPS, 2 * CHUNK], U8, name="y_scales_last", align_bytes=64)
 
-        def quantize_y(s):
+        def quantize_y(s, c0=0, c1=CHUNK):
             c, g = divmod(s, GROUPS)
-            codes = work.tile([P, CHUNK], U32, name="y_codes", align_bytes=64)
-            if c < CHUNKS - 1:
-                scales = y_scales_early[:, g, c * CHUNK:(c + 1) * CHUNK]
+            n0, n1 = c * CHUNK + c0, c * CHUNK + c1
+            codes = work.tile([P, c1 - c0], U32, name="y_codes", align_bytes=64)
+            if n0 < early_cols:
+                scales = y_scales_early[:, g, n0:n1]
             else:
-                scales = y_scales_last[:, g, :]
-            nc.vector.quantize_mx(out=codes[:].bitcast(FP8X4), scales=scales, in_=y_grouped[s][:])
-            dst = out_1[g, :, c * CHUNK:(c + 1) * CHUNK, :].rearrange("p m t -> p (m t)").bitcast(I32)
+                scales = y_scales_last[:, g, n0 - early_cols:n1 - early_cols]
+            nc.vector.quantize_mx(out=codes[:].bitcast(FP8X4), scales=scales,
+                                  in_=y_grouped[s][:, PACK * c0:PACK * c1])
+            dst = out_1[g, :, n0:n1, :].rearrange("p m t -> p (m t)").bitcast(I32)
             nc.sync.dma_start(out=dst, in_=codes[:].bitcast(I32))
 
         def store_scales(engine, scales, c0, c1):
@@ -328,9 +330,11 @@ def tile_tensor_train_weight_merge_b6_kernel(
                 v_q[(s + 1) // 2] = quantize("v", grouped_vs[(s + 1) // 2], work)
             if s >= 2:
                 quantize_y(s - 2)
-            if last:
+            if s == STEPS - 3:
                 store_scales(nc.sync, y_scales_early, 0, early_cols)
-            if s >= 1:
+            if s > STEPS - 3:
+                round_y(nc.scalar.copy, s - 1, 0, SHARE[0])
+            elif s >= 1:
                 round_y(nc.scalar.copy, s - 1)
             if s == 0:
                 wide_b[1] = [widen_rows(b_raw[1, half]) for half in range(2)]
@@ -360,11 +364,14 @@ def tile_tensor_train_weight_merge_b6_kernel(
             if last:
                 gain_vector(s, 256, CHUNK)
                 store_y(s, 256, CHUNK)
+                round_y(nc.scalar.copy, s, 256, CHUNK)
                 gain_vector(s, share, 256)
             else:
                 gain_vector(s, share, CHUNK)
                 if s == STEPS - 2:
                     store_y(s, share, CHUNK)
+                if s >= STEPS - 3:
+                    round_y(nc.scalar.copy, s, share, CHUNK)
                 p_matmul(s + 1, PACK - 1)
                 if s % 2 == 1:
                     spread_gain((s + 1) // 2)
@@ -373,9 +380,8 @@ def tile_tensor_train_weight_merge_b6_kernel(
                 add_p(s + 1, PACK - 1, GATE, CHUNK)
 
         store_y(STEPS - 1, 0, 256)
-        round_y(nc.scalar.copy, STEPS - 1, 384, 512)
-        round_y(nc.vector.tensor_copy, STEPS - 1, 128, 384)
-        round_y(nc.vector.tensor_copy, STEPS - 1, 0, 128)
         quantize_y(STEPS - 2)
-        quantize_y(STEPS - 1)
+        round_y(nc.vector.tensor_copy, STEPS - 1, 0, 256)
+        quantize_y(STEPS - 1, 256, CHUNK)
+        quantize_y(STEPS - 1, 0, 256)
         store_scales(nc.scalar, y_scales_last, early_cols, COLS)

@@ -69,22 +69,22 @@ def tile_tensor_train_weight_merge_b6_kernel(
                         src.rearrange("(p t) n -> p t n", t=PACK))
 
         c_raw, b_raw, a_raw, w_raw = {}, {}, {}, {}
-        c_raw[0] = load_c(0)
         b_raw[0, 0] = load_b(0, 0)
+        c_raw[0] = load_c(0)
+        c_raw[1] = load_c(1)
         c_sc = load(nc.scalar, "c_sc", [P, PACK], F32, C_scale.rearrange("(p t) o -> p (t o)", t=PACK))
         b_sc = load(nc.scalar, "b_sc", [P, PACK], F32, B_scale.rearrange("o (p t) -> p (o t)", t=PACK))
         b_raw[0, 1] = load_b(0, 1)
         a_raw[0, 0] = load_a(0, 0)
         a_raw[0, 1] = load_a(0, 1)
-        a_sc = load(nc.scalar, "a_sc", [P, PACK], F32, A_scale.rearrange("o (p t) -> p (o t)", t=PACK))
-        bond = load(nc.scalar, "bond", [P, PACK], BF16, bond_gain.rearrange("(p t) o -> p (t o)", t=PACK))
-        a_raw[1, 0] = load_a(1, 0)
-        a_raw[1, 1] = load_a(1, 1)
-        c_raw[1] = load_c(1)
+        a_sc = load(nc.sync, "a_sc", [P, PACK], F32, A_scale.rearrange("o (p t) -> p (o t)", t=PACK))
         w_sc = load(nc.sync, "w_sc", [P, GROUPS * PACK * (COLS // BLOCK)], F32,
                     W_scale.rearrange("u v -> (u v)").partition_broadcast(P))
         row_gain = load(nc.sync, "row_gain", [P, GROUPS, PACK], BF16,
                         in_gain.rearrange("(g p t) o -> p g (t o)", p=P, t=PACK))
+        a_raw[1, 0] = load_a(1, 0)
+        a_raw[1, 1] = load_a(1, 1)
+        bond = load(nc.sync, "bond", [P, PACK], BF16, bond_gain.rearrange("(p t) o -> p (t o)", t=PACK))
         w_raw[0, 0] = load_w(0, 0)
         col_gain_p = load(nc.sync, "col_gain_p", [P, CHUNKS, PACK], BF16,
                           out_gain.rearrange("o (c p t) -> p (o c) t", p=P, t=PACK))
@@ -102,16 +102,17 @@ def tile_tensor_train_weight_merge_b6_kernel(
         nblk = COLS // BLOCK
         w_fac = keep.tile([P, GROUPS, PACK, nblk], F32, name="w_fac")
         w_sc_v = w_sc[:].rearrange("p (g q v) -> p g q v", g=GROUPS, q=PACK)
-        for q in range(4):
-            rows = slice(32 * q, 32 * q + 32)
-            nc.gpsimd.tensor_tensor(
-                out=w_fac[rows],
-                in0=w_sc_v[rows, :, q:q + 1, :].to_broadcast([32, GROUPS, PACK, nblk]),
-                in1=row_gain[rows].unsqueeze(3).to_broadcast([32, GROUPS, PACK, nblk]),
-                op=MULT,
-            )
         col_gain_f = keep.tile([P, CHUNKS * PACK], F32, name="col_gain_f")
-        nc.gpsimd.tensor_copy(out=col_gain_f[:], in_=col_gain_p[:].rearrange("p c t -> p (c t)"))
+
+        def prepare_gains():
+            for q in range(4):
+                rows = slice(32 * q, 32 * q + 32)
+                nc.gpsimd.tensor_tensor(
+                    out=w_fac[rows],
+                    in0=w_sc_v[rows, :, q:q + 1, :].to_broadcast([32, GROUPS, PACK, nblk]),
+                    in1=row_gain[rows].unsqueeze(3).to_broadcast([32, GROUPS, PACK, nblk]),
+                    op=MULT,
+                )
 
         def new_wide():
             return work.tile([P, WIDE], BF16, name="wide", bufs=2, align_bytes=64)
@@ -257,52 +258,59 @@ def tile_tensor_train_weight_merge_b6_kernel(
                 dst = out_2[:, 4 * q:4 * q + 4, c0:c1].rearrange("g r n -> r g n").bitcast(I32)
                 engine.dma_start(out=dst, in_=scales[32 * q:32 * q + 4].bitcast(I32))
 
-        wide_b0 = [widen_rows(b_raw[0, half], first=(half == 0)) for half in range(2)]
-        planes = new_wide()
-        for t in range(PACK):
-            nc.vector.tensor_scalar(out=planes[:, t * CHUNK:(t + 1) * CHUNK], in0=c_raw[0][:, t, :].bitcast(FP8),
+        planes = [new_wide(), new_wide()]
+
+        def widen_c(n, t):
+            nc.vector.tensor_scalar(out=planes[n][:, t * CHUNK:(t + 1) * CHUNK], in0=c_raw[n][:, t, :].bitcast(FP8),
                                     scalar1=c_sc[:, t:t + 1], scalar2=None, op0=MULT)
-        grouped_c = new_grouped()
-        dst, src = interleave_views(grouped_c[:], planes[:].rearrange("p (t o) -> p t o", t=PACK))
-        nc.vector.tensor_copy(out=dst, in_=src)
+
+        def group_c(n):
+            grouped = new_grouped()
+            nc.gpsimd.tensor_scalar(out=grouped[:].rearrange("p (o t) -> p o t", t=PACK),
+                                    in0=planes[n][:].rearrange("p (t o) -> p o t", t=PACK),
+                                    scalar1=1.0, scalar2=0.0, op0=MULT, op1=ADD)
+            return grouped
+
+        wide_b0 = [widen_rows(b_raw[0, half], first=(half == 0)) for half in range(2)]
+        for n in range(2):
+            for t in range(PACK - 1):
+                widen_c(n, t)
+        widen_c(0, PACK - 1)
+        grouped_c = group_c(0)
+        prepare_gains()
         banks_b = [turn(wide_b0[half]) for half in range(2)]
         wide_a0 = [widen_rows(a_raw[0, half]) for half in range(2)]
         banks_a = [turn(wide_a0[half]) for half in range(2)]
         wide_a1 = [widen_rows(a_raw[1, half]) for half in range(2)]
+        widen_w(0)
+        nc.scalar.copy(out=col_gain_f[:], in_=col_gain_p[:].rearrange("p c t -> p (c t)"))
+        widen_w(1)
         grouped_b = new_grouped()
         grouped_a = new_grouped()
-        scale_turned(banks_b[0], b_sc, grouped_b, 0)
+        for half in range(2):
+            scale_turned(banks_b[half], b_sc, grouped_b, half)
+        for half in range(2):
+            scale_turned(banks_a[half], a_sc, grouped_a, half)
         c_q[0] = quantize("c0", grouped_c, keep)
-        scale_turned(banks_b[1], b_sc, grouped_b, 1)
-        scale_turned(banks_a[0], a_sc, grouped_a, 0)
         b_q[0] = quantize("b0", grouped_b, keep)
         banks_u = [u_matmuls(0, j) for j in range(4)]
-        scale_turned(banks_a[1], a_sc, grouped_a, 1)
         banks_a = [turn(wide_a1[half]) for half in range(2)]
-
-        planes = new_wide()
-        for t in range(PACK):
-            nc.scalar.activation(out=planes[:, t * CHUNK:(t + 1) * CHUNK], in_=c_raw[1][:, t, :].bitcast(FP8),
-                                 func=COPY, scale=c_sc[:, t:t + 1])
-        grouped_c = new_grouped()
-        dst, src = interleave_views(grouped_c[:], planes[:].rearrange("p (t o) -> p t o", t=PACK))
-        nc.scalar.copy(out=dst, in_=src)
-        widen_w(0)
-        widen_w(1)
+        a_q[0] = quantize("a0", grouped_a, keep)
+        widen_c(1, PACK - 1)
+        grouped_c = group_c(1)
 
         grouped_v = new_grouped()
-        u_out(banks_u[0], grouped_v, 0)
-        a_q[0] = quantize("a0", grouped_a, keep)
-        for j in range(1, 4):
+        for j in range(4):
             u_out(banks_u[j], grouped_v, j)
         grouped_a = new_grouped()
-        scale_turned(banks_a[0], a_sc, grouped_a, 0)
+        for half in range(2):
+            scale_turned(banks_a[half], a_sc, grouped_a, half)
         v_q[0] = quantize("v", grouped_v, work)
         for t in range(PACK):
             p_matmul(0, t)
         spread_gain(0)
-        scale_turned(banks_a[1], a_sc, grouped_a, 1)
         c_q[1] = quantize("c1", grouped_c, keep)
+        a_q[1] = quantize("a1", grouped_a, keep)
         for t in range(PACK - 1):
             add_p(0, t)
         add_p(0, PACK - 1, GATE, CHUNK)
@@ -320,8 +328,6 @@ def tile_tensor_train_weight_merge_b6_kernel(
                 store_y(s - 1, 0, SHARE[0])
             elif s >= 1:
                 store_y(s - 1)
-            if s == 0:
-                a_q[1] = quantize("a1", grouped_a, keep)
             if s == 2:
                 b_q[1] = quantize("b1", grouped_bs[1], keep)
             if s == 5:

@@ -20,14 +20,20 @@ COPY = mybir.ActivationFunctionType.Copy
 
 P = 128
 PACK = 4
+QUADS = 4
 CHUNK = 512
+HALF = CHUNK // 2
+WIDE = PACK * CHUNK
 GROUPS = D_IN // CHUNK
 CHUNKS = COLS // CHUNK
 STEPS = GROUPS * CHUNKS
-WIDE = PACK * CHUNK
+BLOCKS = COLS // BLOCK
+
 GATE = 128
-SHARE = {4: 480, 2: 384, 0: 288}
+SHARE_BASE = 288
+SHARE_PER_JOB = 48
 LAST_SHARE = 128
+SCALAR_U_STEPS = (0, 3, 5)
 
 
 def tile_tensor_train_weight_merge_b6_kernel(
@@ -78,14 +84,16 @@ def tile_tensor_train_weight_merge_b6_kernel(
         a_raw[0, 0] = load_a(0, 0)
         a_raw[0, 1] = load_a(0, 1)
         a_sc = load(nc.sync, "a_sc", [P, PACK], F32, A_scale.rearrange("o (p t) -> p (o t)", t=PACK))
-        w_sc = load(nc.sync, "w_sc", [P, GROUPS * PACK * (COLS // BLOCK)], F32,
-                    W_scale.rearrange("u v -> (u v)").partition_broadcast(P))
-        row_gain = load(nc.sync, "row_gain", [P, GROUPS, PACK], BF16,
-                        in_gain.rearrange("(g p t) o -> p g (t o)", p=P, t=PACK))
         a_raw[1, 0] = load_a(1, 0)
         a_raw[1, 1] = load_a(1, 1)
-        bond = load(nc.sync, "bond", [P, PACK], BF16, bond_gain.rearrange("(p t) o -> p (t o)", t=PACK))
         w_raw[0, 0] = load_w(0, 0)
+        w_sc = keep.tile([P, GROUPS, BLOCKS], F32, name="w_sc")
+        for q in range(QUADS):
+            src = W_scale.rearrange("(g q) v -> q g v", q=QUADS)[q].partition_broadcast(32)
+            nc.sync.dma_start(out=w_sc[32 * q:32 * q + 32], in_=src)
+        row_gain = load(nc.sync, "row_gain", [P, GROUPS, PACK], BF16,
+                        in_gain.rearrange("(g p t) o -> p g (t o)", p=P, t=PACK))
+        bond = load(nc.sync, "bond", [P, PACK], BF16, bond_gain.rearrange("(p t) o -> p (t o)", t=PACK))
         col_gain_p = load(nc.sync, "col_gain_p", [P, CHUNKS, PACK], BF16,
                           out_gain.rearrange("o (c p t) -> p (o c) t", p=P, t=PACK))
         w_raw[1, 0] = load_w(1, 0)
@@ -99,23 +107,8 @@ def tile_tensor_train_weight_merge_b6_kernel(
             for g in range(GROUPS):
                 w_raw[g, h] = load_w(g, h)
 
-        nblk = COLS // BLOCK
-        w_fac = keep.tile([P, GROUPS, PACK, nblk], F32, name="w_fac")
-        w_sc_v = w_sc[:].rearrange("p (g q v) -> p g q v", g=GROUPS, q=PACK)
+        w_fac = keep.tile([P, GROUPS, PACK, BLOCKS], F32, name="w_fac")
         col_gain_f = keep.tile([P, CHUNKS * PACK], F32, name="col_gain_f")
-
-        def prepare_gains():
-            for q in range(4):
-                rows = slice(32 * q, 32 * q + 32)
-                nc.gpsimd.tensor_tensor(
-                    out=w_fac[rows],
-                    in0=w_sc_v[rows, :, q:q + 1, :].to_broadcast([32, GROUPS, PACK, nblk]),
-                    in1=row_gain[rows].unsqueeze(3).to_broadcast([32, GROUPS, PACK, nblk]),
-                    op=MULT,
-                )
-
-        def new_wide():
-            return work.tile([P, WIDE], BF16, name="wide", bufs=2, align_bytes=64)
 
         def new_grouped():
             return work.tile([P, WIDE], BF16, name="grouped", bufs=4, align_bytes=64)
@@ -129,9 +122,9 @@ def tile_tensor_train_weight_merge_b6_kernel(
             nc.vector.quantize_mx(out=codes[:].bitcast(FP8X4), scales=scales[:], in_=grouped[:])
             return codes, scales
 
-        def interleave_views(grouped, planes):
+        def grouping_views(grouped, by_slot):
             dst = grouped.rearrange("p (c i t) -> p c t i", i=4, t=PACK)
-            src = planes.rearrange("p t (c i) -> p c t i", i=4)
+            src = by_slot.rearrange("p t (c i) -> p c t i", i=4)
             return dst, src
 
         def widen_rows(raw, first=False):
@@ -148,15 +141,15 @@ def tile_tensor_train_weight_merge_b6_kernel(
             words = wide[:].bitcast(F32)
             for j in range(2):
                 for u in range(2):
-                    c0 = 256 * u + P * j
-                    nc.tensor.transpose(bank[:, c0:c0 + P], words[:, 256 * j + u:256 * (j + 1):2], ident[:])
+                    c0 = HALF * u + P * j
+                    nc.tensor.transpose(bank[:, c0:c0 + P], words[:, HALF * j + u:HALF * (j + 1):2], ident[:])
             return bank
 
         def scale_turned(bank, scale, grouped, half):
             nc.vector.tensor_tensor(
-                out=grouped[:, 1024 * half:1024 * (half + 1)].rearrange("p (r u e) -> p r u e", u=2, e=2),
+                out=grouped[:, WIDE // 2 * half:WIDE // 2 * (half + 1)].rearrange("p (r u e) -> p r u e", u=2, e=2),
                 in0=bank[:].bitcast(BF16).rearrange("p (u r e) -> p r u e", u=2, e=2),
-                in1=scale[:].rearrange("p (u e) -> p u e", e=2).unsqueeze(1).to_broadcast([P, 256, 2, 2]),
+                in1=scale[:].rearrange("p (u e) -> p u e", e=2).unsqueeze(1).to_broadcast([P, HALF, 2, 2]),
                 op=MULT,
             )
 
@@ -182,6 +175,22 @@ def tile_tensor_train_weight_merge_b6_kernel(
                 in1=bond[:].unsqueeze(1).to_broadcast([P, P, PACK]),
                 op=MULT,
             )
+
+        def u_matmuls_wide(c, half):
+            cols = slice(HALF * half, HALF * (half + 1))
+            pair = [new_bank(), new_bank()]
+            for t in range(PACK):
+                mx(pair[t // 2][:, HALF * (t % 2):HALF * (t % 2 + 1)],
+                   b_q[c // 2], slice(P * t, P * (t + 1)), c_q[c % 2], cols)
+            return pair
+
+        def u_out_scalar(pair, grouped, half):
+            v_slots = work.tile([P, PACK, HALF], BF16, name="v_slots", bufs=2)
+            for t in range(PACK):
+                nc.scalar.activation(out=v_slots[:, t, :], in_=pair[t // 2][:, HALF * (t % 2):HALF * (t % 2 + 1)],
+                                     func=COPY, scale=bond_f[:, t:t + 1])
+            dst, src = grouping_views(grouped[:, PACK * HALF * half:PACK * HALF * (half + 1)], v_slots[:])
+            nc.scalar.copy(out=dst, in_=src)
 
         y, p_bank, gain_bank, y_grouped = {}, {}, {}, {}
 
@@ -210,6 +219,11 @@ def tile_tensor_train_weight_merge_b6_kernel(
                 in1=y[s][:, t, c0:c1], op0=MULT, op1=ADD,
             )
 
+        def add_p_but_gate(s):
+            for t in range(PACK - 1):
+                add_p(s, t)
+            add_p(s, PACK - 1, GATE, CHUNK)
+
         def spread_gain(c):
             gain_bank[c] = gain_psum.tile([P, CHUNK], F32, name="gain_bank")
             for t in range(PACK):
@@ -233,7 +247,7 @@ def tile_tensor_train_weight_merge_b6_kernel(
         def round_y(copy, s, c0=0, c1=CHUNK):
             if s not in y_grouped:
                 y_grouped[s] = work.tile([P, WIDE], BF16, name="y_grouped", align_bytes=64)
-            dst, src = interleave_views(y_grouped[s][:], y[s][:])
+            dst, src = grouping_views(y_grouped[s][:], y[s][:])
             copy(out=dst[:, c0 // 4:c1 // 4], in_=src[:, c0 // 4:c1 // 4])
 
         early_cols = COLS - 2 * CHUNK
@@ -254,140 +268,161 @@ def tile_tensor_train_weight_merge_b6_kernel(
             nc.sync.dma_start(out=dst, in_=codes[:].bitcast(I32))
 
         def store_scales(engine, scales, c0, c1):
-            for q in range(4):
+            for q in range(QUADS):
                 dst = out_2[:, 4 * q:4 * q + 4, c0:c1].rearrange("g r n -> r g n").bitcast(I32)
                 engine.dma_start(out=dst, in_=scales[32 * q:32 * q + 4].bitcast(I32))
 
-        planes = [new_wide(), new_wide()]
+        c_slots = [work.tile([P, WIDE], BF16, name="c_slots", bufs=2, align_bytes=64),
+                   work.tile([P, WIDE], BF16, name="c_slots", bufs=2, align_bytes=64)]
 
         def widen_c(n, t):
-            nc.vector.tensor_scalar(out=planes[n][:, t * CHUNK:(t + 1) * CHUNK], in0=c_raw[n][:, t, :].bitcast(FP8),
+            nc.vector.tensor_scalar(out=c_slots[n][:, t * CHUNK:(t + 1) * CHUNK], in0=c_raw[n][:, t, :].bitcast(FP8),
                                     scalar1=c_sc[:, t:t + 1], scalar2=None, op0=MULT)
 
         def group_c(n):
             grouped = new_grouped()
             nc.gpsimd.tensor_scalar(out=grouped[:].rearrange("p (o t) -> p o t", t=PACK),
-                                    in0=planes[n][:].rearrange("p (t o) -> p o t", t=PACK),
+                                    in0=c_slots[n][:].rearrange("p (t o) -> p o t", t=PACK),
                                     scalar1=1.0, scalar2=0.0, op0=MULT, op1=ADD)
             return grouped
 
-        wide_b0 = [widen_rows(b_raw[0, half], first=(half == 0)) for half in range(2)]
+        wide_b = {0: [widen_rows(b_raw[0, half], first=(half == 0)) for half in range(2)]}
         for n in range(2):
             for t in range(PACK - 1):
                 widen_c(n, t)
         widen_c(0, PACK - 1)
         grouped_c = group_c(0)
-        prepare_gains()
-        banks_b = [turn(wide_b0[half]) for half in range(2)]
+        nc.gpsimd.tensor_tensor(
+            out=w_fac[:],
+            in0=w_sc[:].unsqueeze(2).to_broadcast([P, GROUPS, PACK, BLOCKS]),
+            in1=row_gain[:].unsqueeze(3).to_broadcast([P, GROUPS, PACK, BLOCKS]),
+            op=MULT,
+        )
+        banks_b = [turn(wide_b[0][half]) for half in range(2)]
         wide_a0 = [widen_rows(a_raw[0, half]) for half in range(2)]
         banks_a = [turn(wide_a0[half]) for half in range(2)]
         wide_a1 = [widen_rows(a_raw[1, half]) for half in range(2)]
         widen_w(0)
-        nc.scalar.copy(out=col_gain_f[:], in_=col_gain_p[:].rearrange("p c t -> p (c t)"))
+        bond_f = keep.tile([P, PACK], F32, name="bond_f")
+        nc.scalar.copy(out=bond_f[:], in_=bond[:])
         widen_w(1)
-        grouped_b = new_grouped()
+        wide_b[1] = [widen_rows(b_raw[1, half]) for half in range(2)]
+        nc.scalar.copy(out=col_gain_f[:], in_=col_gain_p[:].rearrange("p c t -> p (c t)"))
+        widen_w(2)
+        grouped_b = {0: new_grouped()}
         grouped_a = new_grouped()
         for half in range(2):
-            scale_turned(banks_b[half], b_sc, grouped_b, half)
+            scale_turned(banks_b[half], b_sc, grouped_b[0], half)
         for half in range(2):
             scale_turned(banks_a[half], a_sc, grouped_a, half)
         c_q[0] = quantize("c0", grouped_c, keep)
-        b_q[0] = quantize("b0", grouped_b, keep)
+        b_q[0] = quantize("b0", grouped_b[0], keep)
         banks_u = [u_matmuls(0, j) for j in range(4)]
         banks_a = [turn(wide_a1[half]) for half in range(2)]
         a_q[0] = quantize("a0", grouped_a, keep)
         widen_c(1, PACK - 1)
         grouped_c = group_c(1)
 
-        grouped_v = new_grouped()
+        grouped_v = {0: new_grouped()}
         for j in range(4):
-            u_out(banks_u[j], grouped_v, j)
+            u_out(banks_u[j], grouped_v[0], j)
         grouped_a = new_grouped()
         for half in range(2):
             scale_turned(banks_a[half], a_sc, grouped_a, half)
-        v_q[0] = quantize("v", grouped_v, work)
+        v_q[0] = quantize("v", grouped_v[0], work)
         for t in range(PACK):
             p_matmul(0, t)
         spread_gain(0)
         c_q[1] = quantize("c1", grouped_c, keep)
         a_q[1] = quantize("a1", grouped_a, keep)
-        for t in range(PACK - 1):
-            add_p(0, t)
-        add_p(0, PACK - 1, GATE, CHUNK)
+        add_p_but_gate(0)
 
         u_jobs = {0: [(1, j) for j in range(4)], 2: [(2, j) for j in range(4)]}
         for c in range(3, CHUNKS):
             u_jobs[2 * c - 3] = [(c, 0), (c, 1)]
             u_jobs[2 * c - 2] = [(c, 2), (c, 3)]
+        scalar_u = {}
+        for s in SCALAR_U_STEPS:
+            c, j = u_jobs[s][-1]
+            scalar_u[s] = (c, j // 2)
+            u_jobs[s] = u_jobs[s][:-2]
         b_jobs = {1: [(1, 0), (1, 1)], 3: [(2, 0)], 4: [(2, 1)]}
-        wide_b, grouped_bs, grouped_vs = {}, {}, {}
+        b_quantised_in = {2: 1, 5: 2}
+        catch_up = SCALAR_U_STEPS[1]
+        split_from = STEPS - 3
 
         for s in range(STEPS):
             last = s == STEPS - 1
             if last:
-                store_y(s - 1, 0, SHARE[0])
+                store_y(s - 1, 0, SHARE_BASE)
             elif s >= 1:
                 store_y(s - 1)
-            if s == 2:
-                b_q[1] = quantize("b1", grouped_bs[1], keep)
-            if s == 5:
-                b_q[2] = quantize("b2", grouped_bs[2], keep)
-            if s % 2 == 1 and (s + 1) // 2 < CHUNKS:
-                v_q[(s + 1) // 2] = quantize("v", grouped_vs[(s + 1) // 2], work)
+
+            if s in b_quantised_in:
+                h = b_quantised_in[s]
+                b_q[h] = quantize("b%d" % h, grouped_b[h], keep)
+            if s % 2 == 1 and not last:
+                v_q[(s + 1) // 2] = quantize("v", grouped_v[(s + 1) // 2], work)
             if s >= 2:
                 quantize_y(s - 2)
-            if s == STEPS - 3:
+            if s - 2 == GROUPS * (early_cols // CHUNK) - 1:
                 store_scales(nc.sync, y_scales_early, 0, early_cols)
-            if s > STEPS - 3:
-                round_y(nc.scalar.copy, s - 1, 0, SHARE[0])
-            elif s >= 1:
-                round_y(nc.scalar.copy, s - 1)
-            if s == 0:
-                wide_b[1] = [widen_rows(b_raw[1, half]) for half in range(2)]
-            if s + 2 < STEPS:
-                widen_w(s + 2)
-            if s == 0:
-                wide_b[2] = [widen_rows(b_raw[2, half]) for half in range(2)]
 
-            jobs = [("u", c, j) for c, j in u_jobs.get(s, [])] + [("b", h, j) for h, j in b_jobs.get(s, [])]
-            weight = sum(1 if kind == "u" else 2 for kind, c, j in jobs)
-            share = LAST_SHARE if last else SHARE[weight]
-            banks = [u_matmuls(c, j) if kind == "u" else turn(wide_b[c][j]) for kind, c, j in jobs]
+            step_u, step_b = u_jobs.get(s, []), b_jobs.get(s, [])
+            banks_u = [u_matmuls(c, j) for c, j in step_u]
+            banks_b = [turn(wide_b[h][half]) for h, half in step_b]
+            if s in scalar_u:
+                pair = u_matmuls_wide(*scalar_u[s])
+            for c in [c for c, j in step_u] + list(scalar_u.get(s, ()))[:1]:
+                if c not in grouped_v:
+                    grouped_v[c] = new_grouped()
+            share = LAST_SHARE if last else SHARE_BASE + SHARE_PER_JOB * (len(step_u) + 2 * len(step_b))
+
             add_p(s, PACK - 1, 0, GATE)
             gain_gpsimd(s, 0, share)
             if not last:
                 for t in range(PACK - 1):
                     p_matmul(s + 1, t)
-            for n, (kind, c, j) in enumerate(jobs):
-                if kind == "u":
-                    if j == 0:
-                        grouped_vs[c] = new_grouped()
-                    u_out(banks[n], grouped_vs[c], j)
-                else:
-                    if j == 0:
-                        grouped_bs[c] = new_grouped()
-                    scale_turned(banks[n], b_sc, grouped_bs[c], j)
+            for bank, (c, j) in zip(banks_u, step_u):
+                u_out(bank, grouped_v[c], j)
+            for bank, (h, half) in zip(banks_b, step_b):
+                if half == 0:
+                    grouped_b[h] = new_grouped()
+                scale_turned(bank, b_sc, grouped_b[h], half)
+
+            if s > split_from:
+                round_y(nc.scalar.copy, s - 1, 0, SHARE_BASE)
+            elif s >= 1:
+                round_y(nc.scalar.copy, s - 1)
+            if s in scalar_u:
+                c, half = scalar_u[s]
+                u_out_scalar(pair, grouped_v[c], half)
+            if s == 0:
+                wide_b[2] = [widen_rows(b_raw[2, half]) for half in range(2)]
+            if s < catch_up:
+                widen_w(s + 3)
+            elif s > catch_up and s + 2 < STEPS:
+                widen_w(s + 2)
+
             if last:
-                gain_vector(s, 256, CHUNK)
-                store_y(s, 256, CHUNK)
-                round_y(nc.scalar.copy, s, 256, CHUNK)
-                gain_vector(s, share, 256)
+                gain_vector(s, HALF, CHUNK)
+                store_y(s, HALF, CHUNK)
+                round_y(nc.scalar.copy, s, HALF, CHUNK)
+                gain_vector(s, share, HALF)
             else:
                 gain_vector(s, share, CHUNK)
                 if s == STEPS - 2:
                     store_y(s, share, CHUNK)
-                if s >= STEPS - 3:
+                if s >= split_from:
                     round_y(nc.scalar.copy, s, share, CHUNK)
                 p_matmul(s + 1, PACK - 1)
                 if s % 2 == 1:
                     spread_gain((s + 1) // 2)
-                for t in range(PACK - 1):
-                    add_p(s + 1, t)
-                add_p(s + 1, PACK - 1, GATE, CHUNK)
+                add_p_but_gate(s + 1)
 
-        store_y(STEPS - 1, 0, 256)
+        store_y(STEPS - 1, 0, HALF)
         quantize_y(STEPS - 2)
-        round_y(nc.vector.tensor_copy, STEPS - 1, 0, 256)
-        quantize_y(STEPS - 1, 256, CHUNK)
-        quantize_y(STEPS - 1, 0, 256)
+        round_y(nc.vector.tensor_copy, STEPS - 1, 0, HALF)
+        quantize_y(STEPS - 1, HALF, CHUNK)
+        quantize_y(STEPS - 1, 0, HALF)
         store_scales(nc.scalar, y_scales_last, early_cols, COLS)

from contextlib import ExitStack

import concourse.mybir as mybir
from concourse.masks import make_identity

D_IN, RANK, HEADS, D_OUT, BLOCK = 1024, 512, 3, 1024, 128
COLS = HEADS * D_OUT
FLOPS = 2 * (HEADS * RANK) * RANK * D_OUT + 2 * D_IN * RANK * COLS

F32 = mybir.dt.float32
BF16 = mybir.dt.bfloat16
U32 = mybir.dt.uint32
I32 = mybir.dt.int32
U8 = mybir.dt.uint8
FP8 = mybir.dt.float8_e4m3fn
FP8X4 = mybir.dt.float8_e4m3fn_x4
MULT = mybir.AluOpType.mult
ADD = mybir.AluOpType.add
COPY = mybir.ActivationFunctionType.Copy

P = 128
PACK = 4
QUADS = 4
CHUNK = 512
HALF = CHUNK // 2
WIDE = PACK * CHUNK
GROUPS = D_IN // CHUNK
CHUNKS = COLS // CHUNK
STEPS = GROUPS * CHUNKS
BLOCKS = COLS // BLOCK

GATE = 128
SHARE_BASE = 288
SHARE_PER_JOB = 48
LAST_SHARE = 128
SCALAR_U_STEPS = (0, 3, 5)


def tile_tensor_train_weight_merge_b6_kernel(
    tc, W_bytes, W_scale, A_bytes, A_scale, B_bytes, B_scale, C_bytes, C_scale,
    bond_gain, in_gain, out_gain, out_0, out_1, out_2,
):
    nc = tc.nc
    with ExitStack() as ctx:
        keep = ctx.enter_context(tc.tile_pool(name="keep", bufs=1))
        work = ctx.enter_context(tc.tile_pool(name="work", bufs=3))
        ypool = ctx.enter_context(tc.tile_pool(name="ypool", bufs=8))
        psum = ctx.enter_context(tc.psum_pool(name="psum", bufs=7))
        gain_psum = ctx.enter_context(tc.psum_pool(name="gain_psum", bufs=1))
        ctx.enter_context(tc.manual_schedule())

        ident = keep.tile([P, P], F32, name="ident")
        make_identity(nc, ident[:])

        def load(engine, name, shape, dtype, src):
            dst = keep.tile(shape, dtype, name=name)
            engine.dma_start(out=dst[:], in_=src)
            return dst

        def load_c(n):
            src = C_bytes[:, n * CHUNK:(n + 1) * CHUNK].rearrange("(p t) o -> p t o", t=PACK)
            return load(nc.sync, "c_raw%d" % n, [P, PACK, CHUNK], U8, src)

        def load_b(h, half):
            src = B_bytes.rearrange("(p t h) k -> h p t k", t=PACK, h=HEADS)[h][:, 2 * half:2 * half + 2, :]
            return load(nc.sync, "b_raw%d_%d" % (h, half), [P, 2, RANK], U8, src)

        def load_a(g, half):
            src = A_bytes[g * CHUNK:(g + 1) * CHUNK, :].rearrange("(p t) k -> p t k", t=PACK)
            return load(nc.sync, "a_raw%d_%d" % (g, half), [P, 2, RANK], U8, src[:, 2 * half:2 * half + 2, :])

        def load_w(g, h):
            src = W_bytes[g * CHUNK:(g + 1) * CHUNK, h * D_OUT:(h + 1) * D_OUT]
            return load(nc.sync, "w_raw%d_%d" % (g, h), [P, PACK, D_OUT], U8,
                        src.rearrange("(p t) n -> p t n", t=PACK))

        c_raw, b_raw, a_raw, w_raw = {}, {}, {}, {}
        b_raw[0, 0] = load_b(0, 0)
        c_raw[0] = load_c(0)
        c_raw[1] = load_c(1)
        c_sc = load(nc.scalar, "c_sc", [P, PACK], F32, C_scale.rearrange("(p t) o -> p (t o)", t=PACK))
        b_sc = load(nc.scalar, "b_sc", [P, PACK], F32, B_scale.rearrange("o (p t) -> p (o t)", t=PACK))
        b_raw[0, 1] = load_b(0, 1)
        a_raw[0, 0] = load_a(0, 0)
        a_raw[0, 1] = load_a(0, 1)
        a_sc = load(nc.sync, "a_sc", [P, PACK], F32, A_scale.rearrange("o (p t) -> p (o t)", t=PACK))
        a_raw[1, 0] = load_a(1, 0)
        a_raw[1, 1] = load_a(1, 1)
        w_raw[0, 0] = load_w(0, 0)
        w_sc = keep.tile([P, GROUPS, BLOCKS], F32, name="w_sc")
        for q in range(QUADS):
            src = W_scale.rearrange("(g q) v -> q g v", q=QUADS)[q].partition_broadcast(32)
            nc.sync.dma_start(out=w_sc[32 * q:32 * q + 32], in_=src)
        row_gain = load(nc.sync, "row_gain", [P, GROUPS, PACK], BF16,
                        in_gain.rearrange("(g p t) o -> p g (t o)", p=P, t=PACK))
        bond = load(nc.sync, "bond", [P, PACK], BF16, bond_gain.rearrange("(p t) o -> p (t o)", t=PACK))
        col_gain_p = load(nc.sync, "col_gain_p", [P, CHUNKS, PACK], BF16,
                          out_gain.rearrange("o (c p t) -> p (o c) t", p=P, t=PACK))
        w_raw[1, 0] = load_w(1, 0)
        b_raw[1, 0] = load_b(1, 0)
        b_raw[1, 1] = load_b(1, 1)
        col_gain = load(nc.sync, "col_gain", [P, COLS], BF16,
                        out_gain.rearrange("o n -> (o n)").partition_broadcast(P))
        b_raw[2, 0] = load_b(2, 0)
        b_raw[2, 1] = load_b(2, 1)
        for h in range(1, HEADS):
            for g in range(GROUPS):
                w_raw[g, h] = load_w(g, h)

        w_fac = keep.tile([P, GROUPS, PACK, BLOCKS], F32, name="w_fac")
        col_gain_f = keep.tile([P, CHUNKS * PACK], F32, name="col_gain_f")

        def new_grouped():
            return work.tile([P, WIDE], BF16, name="grouped", bufs=4, align_bytes=64)

        def new_bank():
            return psum.tile([P, CHUNK], F32, name="bank")

        def quantize(name, grouped, pool):
            codes = pool.tile([P, CHUNK], U32, name=name + "_codes", align_bytes=64)
            scales = pool.tile([P, CHUNK], U8, name=name + "_scales", align_bytes=64)
            nc.vector.quantize_mx(out=codes[:].bitcast(FP8X4), scales=scales[:], in_=grouped[:])
            return codes, scales

        def grouping_views(grouped, by_slot):
            dst = grouped.rearrange("p (c i t) -> p c t i", i=4, t=PACK)
            src = by_slot.rearrange("p t (c i) -> p c t i", i=4)
            return dst, src

        def widen_rows(raw, first=False):
            wide = work.tile([P, WIDE // 2], BF16, name="wide_rows", bufs=6, align_bytes=64)
            src = raw[:].rearrange("p t k -> p (t k)").bitcast(FP8)
            if first:
                nc.scalar.activation(out=wide[:], in_=src, func=COPY)
            else:
                nc.scalar.copy(out=wide[:], in_=src)
            return wide

        def turn(wide):
            bank = new_bank()
            words = wide[:].bitcast(F32)
            for j in range(2):
                for u in range(2):
                    c0 = HALF * u + P * j
                    nc.tensor.transpose(bank[:, c0:c0 + P], words[:, HALF * j + u:HALF * (j + 1):2], ident[:])
            return bank

        def scale_turned(bank, scale, grouped, half):
            nc.vector.tensor_tensor(
                out=grouped[:, WIDE // 2 * half:WIDE // 2 * (half + 1)].rearrange("p (r u e) -> p r u e", u=2, e=2),
                in0=bank[:].bitcast(BF16).rearrange("p (u r e) -> p r u e", u=2, e=2),
                in1=scale[:].rearrange("p (u e) -> p u e", e=2).unsqueeze(1).to_broadcast([P, HALF, 2, 2]),
                op=MULT,
            )

        a_q, b_q, c_q, v_q = {}, {}, {}, {}

        def mx(out, lhs, lcols, rhs, rcols):
            nc.tensor.matmul_mx(
                out=out, lhsT=lhs[0][:, lcols].bitcast(FP8X4), lhsT_scale=lhs[1][:, lcols],
                rhs=rhs[0][:, rcols].bitcast(FP8X4), rhs_scale=rhs[1][:, rcols], start=True, stop=True,
            )

        def u_matmuls(c, j):
            bank = new_bank()
            for t in range(PACK):
                mx(bank[:, P * t:P * (t + 1)], b_q[c // 2], slice(P * t, P * (t + 1)),
                   c_q[c % 2], slice(P * j, P * (j + 1)))
            return bank

        def u_out(bank, grouped, j):
            nc.vector.tensor_tensor(
                out=grouped[:, CHUNK * j:CHUNK * (j + 1)].rearrange("p (o t) -> p o t", t=PACK),
                in0=bank[:].rearrange("p (t o) -> p o t", t=PACK),
                in1=bond[:].unsqueeze(1).to_broadcast([P, P, PACK]),
                op=MULT,
            )

        def u_matmuls_wide(c, half):
            cols = slice(HALF * half, HALF * (half + 1))
            pair = [new_bank(), new_bank()]
            for t in range(PACK):
                mx(pair[t // 2][:, HALF * (t % 2):HALF * (t % 2 + 1)],
                   b_q[c // 2], slice(P * t, P * (t + 1)), c_q[c % 2], cols)
            return pair

        def u_out_scalar(pair, grouped, half):
            v_slots = work.tile([P, PACK, HALF], BF16, name="v_slots", bufs=2)
            for t in range(PACK):
                nc.scalar.activation(out=v_slots[:, t, :], in_=pair[t // 2][:, HALF * (t % 2):HALF * (t % 2 + 1)],
                                     func=COPY, scale=bond_f[:, t:t + 1])
            dst, src = grouping_views(grouped[:, PACK * HALF * half:PACK * HALF * (half + 1)], v_slots[:])
            nc.scalar.copy(out=dst, in_=src)

        y, p_bank, gain_bank, y_grouped = {}, {}, {}, {}

        def widen_w(s):
            c, g = divmod(s, GROUPS)
            y[s] = ypool.tile([P, PACK, CHUNK], F32, name="y")
            raw = w_raw[g, c // 2]
            for t in range(PACK):
                for v in range(CHUNK // BLOCK):
                    c0 = (c % 2) * CHUNK + v * BLOCK
                    blk = c * (CHUNK // BLOCK) + v
                    nc.scalar.activation(
                        out=y[s][:, t, v * BLOCK:(v + 1) * BLOCK], in_=raw[:, t, c0:c0 + BLOCK].bitcast(FP8),
                        func=COPY, scale=w_fac[:, g, t, blk:blk + 1],
                    )

        def p_matmul(s, t):
            c, g = divmod(s, GROUPS)
            p_bank[s, t] = new_bank()
            mx(p_bank[s, t][:], a_q[g], slice(P * t, P * (t + 1)), v_q[c], slice(0, CHUNK))

        def add_p(s, t, c0=0, c1=CHUNK):
            g = s % GROUPS
            nc.vector.scalar_tensor_tensor(
                out=y[s][:, t, c0:c1], in0=p_bank[s, t][:, c0:c1], scalar=row_gain[:, g, t:t + 1],
                in1=y[s][:, t, c0:c1], op0=MULT, op1=ADD,
            )

        def add_p_but_gate(s):
            for t in range(PACK - 1):
                add_p(s, t)
            add_p(s, PACK - 1, GATE, CHUNK)

        def spread_gain(c):
            gain_bank[c] = gain_psum.tile([P, CHUNK], F32, name="gain_bank")
            for t in range(PACK):
                col = col_gain_f[:, PACK * c + t:PACK * c + t + 1].to_broadcast([P, P])
                nc.tensor.transpose(gain_bank[c][:, t:CHUNK:PACK], col, ident[:])

        def gain_gpsimd(s, c0, c1):
            c = s // GROUPS
            gain = col_gain[:, c * CHUNK + c0:c * CHUNK + c1].unsqueeze(1).to_broadcast([P, PACK, c1 - c0])
            nc.gpsimd.tensor_tensor(out=y[s][:, :, c0:c1], in0=y[s][:, :, c0:c1], in1=gain, op=MULT)

        def gain_vector(s, c0, c1):
            gain = gain_bank[s // GROUPS][:, c0:c1].unsqueeze(1).to_broadcast([P, PACK, c1 - c0])
            nc.vector.tensor_tensor(out=y[s][:, :, c0:c1], in0=y[s][:, :, c0:c1], in1=gain, op=MULT)

        def store_y(s, c0=0, c1=CHUNK):
            c, g = divmod(s, GROUPS)
            dst = out_0[g * CHUNK:(g + 1) * CHUNK, c * CHUNK + c0:c * CHUNK + c1]
            nc.sync.dma_start(out=dst.rearrange("(p t) n -> p t n", t=PACK), in_=y[s][:, :, c0:c1])

        def round_y(copy, s, c0=0, c1=CHUNK):
            if s not in y_grouped:
                y_grouped[s] = work.tile([P, WIDE], BF16, name="y_grouped", align_bytes=64)
            dst, src = grouping_views(y_grouped[s][:], y[s][:])
            copy(out=dst[:, c0 // 4:c1 // 4], in_=src[:, c0 // 4:c1 // 4])

        early_cols = COLS - 2 * CHUNK
        y_scales_early = keep.tile([P, GROUPS, early_cols], U8, name="y_scales_early", align_bytes=64)
        y_scales_last = keep.tile([P, GROUPS, 2 * CHUNK], U8, name="y_scales_last", align_bytes=64)

        def quantize_y(s, c0=0, c1=CHUNK):
            c, g = divmod(s, GROUPS)
            n0, n1 = c * CHUNK + c0, c * CHUNK + c1
            codes = work.tile([P, c1 - c0], U32, name="y_codes", align_bytes=64)
            if n0 < early_cols:
                scales = y_scales_early[:, g, n0:n1]
            else:
                scales = y_scales_last[:, g, n0 - early_cols:n1 - early_cols]
            nc.vector.quantize_mx(out=codes[:].bitcast(FP8X4), scales=scales,
                                  in_=y_grouped[s][:, PACK * c0:PACK * c1])
            dst = out_1[g, :, n0:n1, :].rearrange("p m t -> p (m t)").bitcast(I32)
            nc.sync.dma_start(out=dst, in_=codes[:].bitcast(I32))

        def store_scales(engine, scales, c0, c1):
            for q in range(QUADS):
                dst = out_2[:, 4 * q:4 * q + 4, c0:c1].rearrange("g r n -> r g n").bitcast(I32)
                engine.dma_start(out=dst, in_=scales[32 * q:32 * q + 4].bitcast(I32))

        c_slots = [work.tile([P, WIDE], BF16, name="c_slots", bufs=2, align_bytes=64),
                   work.tile([P, WIDE], BF16, name="c_slots", bufs=2, align_bytes=64)]

        def widen_c(n, t):
            nc.vector.tensor_scalar(out=c_slots[n][:, t * CHUNK:(t + 1) * CHUNK], in0=c_raw[n][:, t, :].bitcast(FP8),
                                    scalar1=c_sc[:, t:t + 1], scalar2=None, op0=MULT)

        def group_c(n):
            grouped = new_grouped()
            nc.gpsimd.tensor_scalar(out=grouped[:].rearrange("p (o t) -> p o t", t=PACK),
                                    in0=c_slots[n][:].rearrange("p (t o) -> p o t", t=PACK),
                                    scalar1=1.0, scalar2=0.0, op0=MULT, op1=ADD)
            return grouped

        wide_b = {0: [widen_rows(b_raw[0, half], first=(half == 0)) for half in range(2)]}
        for n in range(2):
            for t in range(PACK - 1):
                widen_c(n, t)
        widen_c(0, PACK - 1)
        grouped_c = group_c(0)
        nc.gpsimd.tensor_tensor(
            out=w_fac[:],
            in0=w_sc[:].unsqueeze(2).to_broadcast([P, GROUPS, PACK, BLOCKS]),
            in1=row_gain[:].unsqueeze(3).to_broadcast([P, GROUPS, PACK, BLOCKS]),
            op=MULT,
        )
        banks_b = [turn(wide_b[0][half]) for half in range(2)]
        wide_a0 = [widen_rows(a_raw[0, half]) for half in range(2)]
        banks_a = [turn(wide_a0[half]) for half in range(2)]
        wide_a1 = [widen_rows(a_raw[1, half]) for half in range(2)]
        widen_w(0)
        bond_f = keep.tile([P, PACK], F32, name="bond_f")
        nc.scalar.copy(out=bond_f[:], in_=bond[:])
        widen_w(1)
        wide_b[1] = [widen_rows(b_raw[1, half]) for half in range(2)]
        nc.scalar.copy(out=col_gain_f[:], in_=col_gain_p[:].rearrange("p c t -> p (c t)"))
        widen_w(2)
        grouped_b = {0: new_grouped()}
        grouped_a = new_grouped()
        for half in range(2):
            scale_turned(banks_b[half], b_sc, grouped_b[0], half)
        for half in range(2):
            scale_turned(banks_a[half], a_sc, grouped_a, half)
        c_q[0] = quantize("c0", grouped_c, keep)
        b_q[0] = quantize("b0", grouped_b[0], keep)
        banks_u = [u_matmuls(0, j) for j in range(4)]
        banks_a = [turn(wide_a1[half]) for half in range(2)]
        a_q[0] = quantize("a0", grouped_a, keep)
        widen_c(1, PACK - 1)
        grouped_c = group_c(1)

        grouped_v = {0: new_grouped()}
        for j in range(4):
            u_out(banks_u[j], grouped_v[0], j)
        grouped_a = new_grouped()
        for half in range(2):
            scale_turned(banks_a[half], a_sc, grouped_a, half)
        v_q[0] = quantize("v", grouped_v[0], work)
        for t in range(PACK):
            p_matmul(0, t)
        spread_gain(0)
        c_q[1] = quantize("c1", grouped_c, keep)
        a_q[1] = quantize("a1", grouped_a, keep)
        add_p_but_gate(0)

        u_jobs = {0: [(1, j) for j in range(4)], 2: [(2, j) for j in range(4)]}
        for c in range(3, CHUNKS):
            u_jobs[2 * c - 3] = [(c, 0), (c, 1)]
            u_jobs[2 * c - 2] = [(c, 2), (c, 3)]
        scalar_u = {}
        for s in SCALAR_U_STEPS:
            c, j = u_jobs[s][-1]
            scalar_u[s] = (c, j // 2)
            u_jobs[s] = u_jobs[s][:-2]
        b_jobs = {1: [(1, 0), (1, 1)], 3: [(2, 0)], 4: [(2, 1)]}
        b_quantised_in = {2: 1, 5: 2}
        catch_up = SCALAR_U_STEPS[1]
        split_from = STEPS - 3

        for s in range(STEPS):
            last = s == STEPS - 1
            if last:
                store_y(s - 1, 0, SHARE_BASE)
            elif s >= 1:
                store_y(s - 1)

            if s in b_quantised_in:
                h = b_quantised_in[s]
                b_q[h] = quantize("b%d" % h, grouped_b[h], keep)
            if s % 2 == 1 and not last:
                v_q[(s + 1) // 2] = quantize("v", grouped_v[(s + 1) // 2], work)
            if s >= 2:
                quantize_y(s - 2)
            if s - 2 == GROUPS * (early_cols // CHUNK) - 1:
                store_scales(nc.sync, y_scales_early, 0, early_cols)

            step_u, step_b = u_jobs.get(s, []), b_jobs.get(s, [])
            banks_u = [u_matmuls(c, j) for c, j in step_u]
            banks_b = [turn(wide_b[h][half]) for h, half in step_b]
            if s in scalar_u:
                pair = u_matmuls_wide(*scalar_u[s])
            for c in [c for c, j in step_u] + list(scalar_u.get(s, ()))[:1]:
                if c not in grouped_v:
                    grouped_v[c] = new_grouped()
            share = LAST_SHARE if last else SHARE_BASE + SHARE_PER_JOB * (len(step_u) + 2 * len(step_b))

            add_p(s, PACK - 1, 0, GATE)
            gain_gpsimd(s, 0, share)
            if not last:
                for t in range(PACK - 1):
                    p_matmul(s + 1, t)
            for bank, (c, j) in zip(banks_u, step_u):
                u_out(bank, grouped_v[c], j)
            for bank, (h, half) in zip(banks_b, step_b):
                if half == 0:
                    grouped_b[h] = new_grouped()
                scale_turned(bank, b_sc, grouped_b[h], half)

            if s > split_from:
                round_y(nc.scalar.copy, s - 1, 0, SHARE_BASE)
            elif s >= 1:
                round_y(nc.scalar.copy, s - 1)
            if s in scalar_u:
                c, half = scalar_u[s]
                u_out_scalar(pair, grouped_v[c], half)
            if s == 0:
                wide_b[2] = [widen_rows(b_raw[2, half]) for half in range(2)]
            if s < catch_up:
                widen_w(s + 3)
            elif s > catch_up and s + 2 < STEPS:
                widen_w(s + 2)

            if last:
                gain_vector(s, HALF, CHUNK)
                store_y(s, HALF, CHUNK)
                round_y(nc.scalar.copy, s, HALF, CHUNK)
                gain_vector(s, share, HALF)
            else:
                gain_vector(s, share, CHUNK)
                if s == STEPS - 2:
                    store_y(s, share, CHUNK)
                if s >= split_from:
                    round_y(nc.scalar.copy, s, share, CHUNK)
                p_matmul(s + 1, PACK - 1)
                if s % 2 == 1:
                    spread_gain((s + 1) // 2)
                add_p_but_gate(s + 1)

        store_y(STEPS - 1, 0, HALF)
        quantize_y(STEPS - 2)
        round_y(nc.vector.tensor_copy, STEPS - 1, 0, HALF)
        quantize_y(STEPS - 1, HALF, CHUNK)
        quantize_y(STEPS - 1, 0, HALF)
        store_scales(nc.scalar, y_scales_last, early_cols, COLS)
